import numpy as np
import ml_dtypes


def mxq(x, axis, fmt="e4m3"):
    dtype, down = {"e4m3": (ml_dtypes.float8_e4m3fn, 7), "e5m2": (ml_dtypes.float8_e5m2, 14)}[fmt]
    v = np.moveaxis(np.asarray(x, np.float32).astype(ml_dtypes.bfloat16).astype(np.float64), axis, -1)
    blocks = v.reshape(v.shape[:-1] + (-1, 32))
    amax = np.abs(blocks).max(-1, keepdims=True)
    byte = np.maximum(np.where(amax > 0, np.frexp(amax)[1] - 1 + 127, 0) - down, 1)
    scale = np.exp2(byte - 127.0)
    codes = (blocks / scale).astype(np.float32).astype(dtype).astype(np.float64)
    return np.moveaxis((codes * scale).reshape(v.shape), -1, axis)


WIDE = False


def mx_kscale(k):
    if not WIDE:
        return np.ones(k)
    levels = np.array([10, -10, 5, -5, 0])
    if k % 512:
        return np.exp2(np.random.permutation(np.resize(levels, k // 32))).repeat(32)
    a = np.empty((k // 512, 16))
    for p in range(k // 512):
        a[p, :8] = np.random.permutation(np.resize(levels, 8))
        for g in range(8):
            far = levels[np.abs(levels - a[p, g]) >= 10]
            a[p, g + 8] = far[np.random.randint(len(far))]
    return np.exp2(a.ravel()).repeat(32)


def f64(x):
    return np.asarray(x).astype(np.float64)


def striped(idx):
    return np.tile(idx.reshape(-1, 16).T, (8, 1)).astype(np.uint16)


def unstriped(offs):
    return offs[:16].T.reshape(-1).astype(np.int64)


def pack_weight(w):
    k, n = w.shape
    w = f64(np.asarray(w, np.float32).astype(ml_dtypes.bfloat16)).reshape(k // 32, 32, n)
    amax = np.abs(w).max(1)
    byte = np.clip(np.where(amax > 0, np.frexp(amax)[1] - 1 + 127 - 7, 1), 1, 254)
    scaled = (w * np.exp2(127.0 - byte)[:, None, :]).reshape(k, n).astype(np.float32)
    words = np.ascontiguousarray(scaled.reshape(k // 512, 128, 4, n).transpose(0, 1, 3, 2)).astype(ml_dtypes.float8_e4m3fn).view(np.uint8)
    return words, np.ascontiguousarray(byte.astype(np.uint8).reshape(k // 512, 16, n))


def unpack_weight(words, scales):
    g, p, n, _ = words.shape
    vals = np.ascontiguousarray(words).view(ml_dtypes.float8_e4m3fn).astype(np.float64) * np.repeat(np.exp2(scales.astype(np.float64) - 127.0), 8, axis=1)[..., None]
    return vals.transpose(0, 1, 3, 2).reshape(g * 512, n)


def sigmoid(v):
    return 1.0 / (1.0 + np.exp(-np.maximum(v, -700.0)))


K, T, S, V, N, H = 512, 2048, 512, 512, 512, 512


def setup_inputs():
    n = np.random.standard_normal
    s = mx_kscale(K)[:, None]
    u = mx_kscale(S)
    packed_xT = pack_weight(n((K, T)) * s)
    return {
        "x_words": packed_xT[0],
        "x_scales": packed_xT[1],
        "w1": (n((K, H)) / np.sqrt(K) / s).astype(np.float32),
        "w2": (n((K, H)) / np.sqrt(K) / s).astype(np.float32),
        "gk": (np.random.uniform(0.5, 1.5, (H, 1)) * u[:, None]).astype(np.float32),
        "gq": (np.random.uniform(0.5, 1.5, (H, 1)) / u[:, None]).astype(np.float32),
        "wv": (n((K, N)) / np.sqrt(K) / s).astype(np.float32),
        "gi": (np.random.uniform(0.5, 1.5, (S, 1)) / u[:, None]).astype(np.float32),
        "res": n((N, V)).astype(np.float32),
        "gt": (np.random.uniform(0.5, 1.5, (S, 1)) * u[:, None]).astype(np.float32),
        "offs": striped(np.random.permutation(T)[:S]),
        "qs": striped(np.random.permutation(T)[:V]),
    }


def reference(x_words, x_scales, w1, w2, gk, gq, wv, gi, res, gt, offs, qs):
    xq = unpack_weight(x_words, x_scales)[:, unstriped(offs)]
    val = xq.T @ mxq(f64(wv), 0, "e4m3")
    zv = f64(gi) * val
    kf = mxq(f64(w1), 0, "e4m3").T @ xq
    z = f64(gk) * kf
    x_qs = unpack_weight(x_words, x_scales)[:, unstriped(qs)]
    qf = mxq(f64(w2), 0, "e4m3").T @ x_qs
    z2 = f64(gq) * qf
    s = 0.0625 * ((mxq(z, 0, "e4m3").T @ mxq(z2, 0, "e4m3")))
    zp = f64(gt) * sigmoid(s)
    return f64(res) + 0.0625 * ((mxq(zv, 0, "e4m3").T @ mxq(zp, 0, "e4m3")))

@@ -1,0 +1,198 @@
+from contextlib import ExitStack
+
+import concourse.mybir as mybir
+from concourse.masks import make_identity
+
+F32 = mybir.dt.float32
+BF16 = mybir.dt.bfloat16
+I32 = mybir.dt.int32
+U32 = mybir.dt.uint32
+U16 = mybir.dt.uint16
+U8 = mybir.dt.uint8
+FP8X4 = mybir.dt.float8_e4m3fn_x4
+ACT = mybir.ActivationFunctionType
+ALU = mybir.AluOpType
+
+P = 128
+T = 2048
+W = 512
+CH = 128
+FLOPS = 5 * 2 * 512 * 512 * 512
+ZP_MODES = ("S","S","S","V")
+
+
+def tile_picked_listattn_sigmoid_p_kernel(
+    tc, x_words, x_scales, w1, w2, gk, gq, wv, gi, res, gt, offs, qs, out
+):
+    nc = tc.nc
+    with ExitStack() as ctx:
+        keep = ctx.enter_context(tc.tile_pool(name="keep", bufs=1))
+        psum = ctx.enter_context(tc.psum_pool(name="psum", bufs=1))
+
+        def sb(name, shape, dtype):
+            return keep.tile(shape, dtype, name=name, align_bytes=64)
+
+        def bank(b, name):
+            return psum.tile([P, W], F32, name=name, tag="bank%d" % b)
+
+        offs_t = sb("offs_t", [P, W // 16], U16)
+        qs_t = sb("qs_t", [P, W // 16], U16)
+        xw = sb("xw", [P, T], U32)
+        xs = sb("xs", [P, T], U8)
+        nc.vector.memset(xs[:].bitcast(I32), 0)
+        nc.sync.dma_start(xw[:].bitcast(I32), x_words[0].rearrange("p n t -> p (n t)").bitcast(I32))
+        nc.sync.dma_start(offs_t[:], offs)
+        nc.sync.dma_start(qs_t[:], qs)
+        for q in range(4):
+            nc.sync.dma_start(xs[32 * q : 32 * q + 4, :].bitcast(I32), x_scales[0][4 * q : 4 * q + 4, :].bitcast(I32))
+        raw = {name: sb("raw_" + name, [P, 4, W], F32) for name in ("w1", "w2", "wv")}
+        rows = sb("rows", [P, W], F32)
+        nc.sync.dma_start(raw["w1"][:], w1.rearrange("(p j) c -> p j c", j=4))
+        for v, g in enumerate((gk, gq, gi, gt)):
+            nc.sync.dma_start(rows[v : v + 1, :], g.rearrange("k o -> o k"))
+        nc.sync.dma_start(raw["w2"][:], w2.rearrange("(p j) c -> p j c", j=4))
+        nc.sync.dma_start(raw["wv"][:], wv.rearrange("(p j) c -> p j c", j=4))
+        res_t = sb("res_t", [P, 4, W], F32)
+        nc.sync.dma_start(res_t[:], res.rearrange("(a p) v -> p a v", p=P))
+
+        dealt = sb("dealt", [P, W], F32)
+        ident = sb("ident", [P, P], F32)
+        nc.gpsimd.memset(dealt[:], 0.0)
+        make_identity(nc, ident[:])
+        warm = sb("warm", [P, 1], F32)
+        nc.scalar.activation(warm[:], ident[:, 0:1], ACT.Sigmoid)
+        nc.gpsimd.tensor_copy(dealt[0:4, :].rearrange("v (t g i) -> v t g i", t=4, i=4),
+                              rows[0:4, :].rearrange("v (g t i) -> v t g i", t=4, i=4))
+        rows_ps = bank(7, "rows_ps")
+        for t in range(4):
+            nc.tensor.transpose(rows_ps[:, P * t : P * (t + 1)], dealt[:, P * t : P * (t + 1)], ident[:])
+        fac = sb("fac", [P, 16], F32)
+        nc.scalar.copy(fac[:].rearrange("p (v t) -> p v t", t=4), rows_ps[:].rearrange("p (t v) -> p v t", t=4)[:, 0:4, :])
+        GK, GQ, GI, GT = 0, 4, 8, 12
+
+        ko_w = sb("ko_w", [P, W], U32)
+        ko_s_list = sb("ko_s_list", [P, W], U8)
+        ko_s = sb("ko_s", [P, W], U8)
+        qo_w = sb("qo_w", [P, W], U32)
+        qo_s = sb("qo_s", [P, W], U8)
+        nc.vector.tensor_copy(ko_w[:].rearrange("p (t g i) -> p g t i", t=4, i=4), xw[:].indirect(offs_t[:]))
+        nc.vector.tensor_copy(qo_w[:], xw[:].indirect(qs_t[:]))
+        nc.vector.tensor_copy(ko_s_list[:], xs[:].indirect(offs_t[:]))
+        nc.vector.tensor_copy(qo_s[:], xs[:].indirect(qs_t[:]))
+        nc.vector.tensor_copy(
+            ko_s[:].bitcast(I32).rearrange("p (t g) -> p t g", t=4),
+            ko_s_list[:].bitcast(I32).rearrange("p (g t) -> p t g", t=4),
+        )
+
+        def operand(name):
+            return (sb(name + "_b", [P, 4 * W], BF16), sb(name + "_w", [P, W], U32), sb(name + "_s", [P, W], U8))
+
+        def quant(op, c0, c1):
+            nc.vector.quantize_mx(out=op[1][:, c0:c1].bitcast(FP8X4), scales=op[2][:, c0:c1], in_=op[0][:, 4 * c0 : 4 * c1])
+
+        def mm(o, lhs, l0, rhs, r0, r1):
+            nc.tensor.matmul_mx(out=o, lhsT=lhs[1][:, l0 : l0 + P].bitcast(FP8X4), lhsT_scale=lhs[2][:, l0 : l0 + P],
+                                rhs=rhs[1][:, r0:r1].bitcast(FP8X4), rhs_scale=rhs[2][:, r0:r1], start=True, stop=True)
+
+        def cast_dealt(op, name):
+            nc.scalar.copy(op[0][:].rearrange("p (t g i j) -> p t g j i", t=4, i=4, j=4),
+                           raw[name][:].rearrange("p j (g t i) -> p t g j i", t=4, i=4))
+
+        def cast_plain(op, name):
+            nc.scalar.copy(op[0][:].rearrange("p (c i j) -> p c j i", i=4, j=4),
+                           raw[name][:].rearrange("p j (c i) -> p c j i", i=4))
+
+        def direct(op, c, src, f0):
+            nc.vector.tensor_tensor(
+                op[0][:, 4 * CH * c : 4 * CH * (c + 1)].rearrange("p (s t) -> p s t", t=4),
+                src,
+                fac[:, f0 : f0 + 4].unsqueeze(1).to_broadcast([P, CH, 4]),
+                ALU.mult,
+            )
+
+        def weave(op, c0, c1, planes):
+            nc.vector.tensor_copy(op[0][:, 4 * c0 : 4 * c1].rearrange("p (c i t) -> p c t i", i=4, t=4),
+                                  planes.rearrange("p t (c i) -> p c t i", i=4))
+
+        keys = (None, ko_w, ko_s)
+        quer = (None, qo_w, qo_s)
+        w1q, w2q, wvq = operand("w1q"), operand("w2q"), operand("wvq")
+        z, z2, zv, zp = operand("z"), operand("z2"), operand("zv"), operand("zp")
+
+        cast_dealt(w1q, "w1")
+        quant(w1q, 0, W)
+        cast_dealt(w2q, "w2")
+        kf = [bank(c, "kf%d" % c) for c in range(4)]
+        for c in range(4):
+            for t in range(4):
+                mm(kf[c][:, CH * t : CH * (t + 1)], w1q, P * t, keys, CH * c, CH * (c + 1))
+        direct(z, 0, kf[0][:].rearrange("p (t s) -> p s t", t=4), GK)
+        direct(z, 1, kf[1][:].rearrange("p (t s) -> p s t", t=4), GK)
+        quant(w2q, 0, W)
+        cast_plain(wvq, "wv")
+        direct(z, 2, kf[2][:].rearrange("p (t s) -> p s t", t=4), GK)
+        direct(z, 3, kf[3][:].rearrange("p (t s) -> p s t", t=4), GK)
+        z2_planes = []
+        for h in range(2):
+            pl = sb("z2_planes%d" % h, [P, 4, 256], BF16)
+            z2_planes.append(pl)
+            for u in range(2):
+                b = bank(4 + 2 * h + u, "qf%d%d" % (h, u))
+                for e in range(2):
+                    mm(b[:, 256 * e : 256 * (e + 1)], w2q, P * (2 * u + e), quer, 256 * h, 256 * (h + 1))
+                for e in range(2):
+                    t = 2 * u + e
+                    nc.scalar.activation(pl[:, t, :], b[:, 256 * e : 256 * (e + 1)], ACT.Copy, scale=fac[:, GQ + t : GQ + t + 1])
+        quant(wvq, 0, W)
+        quant(z, 0, W)
+        val = [bank(c, "val%d" % c) for c in range(4)]
+        for c in range(4):
+            for t in range(4):
+                mm(val[c][:, CH * t : CH * (t + 1)], keys, P * t, wvq, CH * c, CH * (c + 1))
+        weave(z2, 0, 256, z2_planes[0][:])
+        direct(zv, 0, val[0][:].rearrange("p (t s) -> p s t", t=4), GI)
+        quant(z2, 0, 256)
+        direct(zv, 1, val[1][:].rearrange("p (t s) -> p s t", t=4), GI)
+        weave(z2, 256, 512, z2_planes[1][:])
+        direct(zv, 2, val[2][:].rearrange("p (t s) -> p s t", t=4), GI)
+        quant(z2, 256, 512)
+        direct(zv, 3, val[3][:].rearrange("p (t s) -> p s t", t=4), GI)
+
+        def scores(c):
+            b = bank(4 + c, "s%d" % c)
+            for t in range(4):
+                mm(b[:, CH * t : CH * (t + 1)], z, P * t, z2, CH * c, CH * (c + 1))
+            sg = sb("sg%d" % c, [P, W], F32)
+            if ZP_MODES[c] == "V":
+                nc.scalar.activation(sg[:].rearrange("p (s t) -> p s t", t=4), b[:].rearrange("p (t s) -> p s t", t=4), ACT.Sigmoid, scale=0.0625)
+                return sg
+            nc.scalar.activation(sg[:], b[:], ACT.Sigmoid, scale=0.0625)
+            pl = sb("zp_planes%d" % c, [P, 4, CH], BF16)
+            for t in range(4):
+                nc.scalar.activation(pl[:, t, :], sg[:, CH * t : CH * (t + 1)], ACT.Copy, scale=fac[:, GT + t : GT + t + 1])
+            return pl
+
+        def make_zp(c, src):
+            if ZP_MODES[c] == "V":
+                direct(zp, c, src[:].rearrange("p (s t) -> p s t", t=4), GT)
+            else:
+                weave(zp, CH * c, CH * (c + 1), src[:])
+
+        def finish(c):
+            b = bank(c, "o%d" % c)
+            for a in range(4):
+                mm(b[:, CH * a : CH * (a + 1)], zv, P * a, zp, CH * c, CH * (c + 1))
+            o = sb("o%d" % c, [P, 4, CH], F32)
+            nc.vector.scalar_tensor_tensor(o[:], b[:].rearrange("p (a v) -> p a v", a=4), 0.0625,
+                                           res_t[:, :, CH * c : CH * (c + 1)], ALU.mult, ALU.add)
+            nc.sync.dma_start(out.rearrange("(a p) v -> p a v", p=P)[:, :, CH * c : CH * (c + 1)], o[:])
+
+        made = [scores(c) for c in range(4)]
+        make_zp(0, made[0])
+        quant(zv, 0, W)
+        quant(zp, 0, CH)
+        for c in range(1, 4):
+            make_zp(c, made[c])
+            finish(c - 1)
+            quant(zp, CH * c, CH * (c + 1))
+        finish(3)

@@ -14,11 +14,16 @@ ACT = mybir.ActivationFunctionType
 ALU = mybir.AluOpType
 
 P = 128
-T = 2048
+TOKENS = 2048
 W = 512
-CH = 128
-FLOPS = 5 * 2 * 512 * 512 * 512
-ZP_MODES = ("S","S","S","V")
+SLOTS = 4
+RUN = 4
+HALF = W // 2
+QUARTER = W // 4
+SIXTEENTH = 0.0625
+FLOPS = 5 * 2 * W * W * W
+
+GK, GQ, GI, GT = 0, 4, 8, 12
 
 
 def tile_picked_listattn_sigmoid_p_kernel(
@@ -29,170 +34,253 @@ def tile_picked_listattn_sigmoid_p_kernel(
         keep = ctx.enter_context(tc.tile_pool(name="keep", bufs=1))
         psum = ctx.enter_context(tc.psum_pool(name="psum", bufs=1))
 
-        def sb(name, shape, dtype):
-            return keep.tile(shape, dtype, name=name, align_bytes=64)
+        def sb(name, shape, dtype, tag=None):
+            return keep.tile(shape, dtype, name=name, tag=tag or name, align_bytes=64)
 
         def bank(b, name):
             return psum.tile([P, W], F32, name=name, tag="bank%d" % b)
 
         offs_t = sb("offs_t", [P, W // 16], U16)
         qs_t = sb("qs_t", [P, W // 16], U16)
-        xw = sb("xw", [P, T], U32)
-        xs = sb("xs", [P, T], U8)
-        nc.vector.memset(xs[:].bitcast(I32), 0)
-        nc.sync.dma_start(xw[:].bitcast(I32), x_words[0].rearrange("p n t -> p (n t)").bitcast(I32))
+        table_words = sb("table_words", [P, TOKENS], U32)
+        table_scales = sb("table_scales", [P, TOKENS], U8)
+        nc.vector.memset(table_scales[:].bitcast(I32), 0)
         nc.sync.dma_start(offs_t[:], offs)
         nc.sync.dma_start(qs_t[:], qs)
+        nc.sync.dma_start(table_words[:].bitcast(I32), x_words[0].rearrange("p n t -> p (n t)").bitcast(I32))
         for q in range(4):
-            nc.sync.dma_start(xs[32 * q : 32 * q + 4, :].bitcast(I32), x_scales[0][4 * q : 4 * q + 4, :].bitcast(I32))
-        raw = {name: sb("raw_" + name, [P, 4, W], F32) for name in ("w1", "w2", "wv")}
-        rows = sb("rows", [P, W], F32)
-        nc.sync.dma_start(raw["w1"][:], w1.rearrange("(p j) c -> p j c", j=4))
-        for v, g in enumerate((gk, gq, gi, gt)):
-            nc.sync.dma_start(rows[v : v + 1, :], g.rearrange("k o -> o k"))
-        nc.sync.dma_start(raw["w2"][:], w2.rearrange("(p j) c -> p j c", j=4))
-        nc.sync.dma_start(raw["wv"][:], wv.rearrange("(p j) c -> p j c", j=4))
+            nc.sync.dma_start(
+                table_scales[32 * q + 4 : 32 * q + 8, :].bitcast(I32), x_scales[0][4 * q : 4 * q + 4, :].bitcast(I32)
+            )
+        factor_rows = sb("factor_rows", [P, W], F32)
+        for v, vector in enumerate((gk, gq, gi, gt)):
+            nc.scalar.dma_start(factor_rows[v : v + 1, :], vector.rearrange("k o -> o k"))
+        raw = {}
+        for name, w in (("w1", w1), ("w2", w2), ("wv", wv)):
+            for h in range(2):
+                raw[name, h] = sb("raw_%s%d" % (name, h), [P, SLOTS, HALF], F32)
+                nc.sync.dma_start(
+                    raw[name, h][:], w.rearrange("(p j) c -> p j c", j=SLOTS)[:, :, HALF * h : HALF * (h + 1)]
+                )
         res_t = sb("res_t", [P, 4, W], F32)
         nc.sync.dma_start(res_t[:], res.rearrange("(a p) v -> p a v", p=P))
 
-        dealt = sb("dealt", [P, W], F32)
+        dealt_rows = sb("dealt_rows", [P, W], F32)
         ident = sb("ident", [P, P], F32)
-        nc.gpsimd.memset(dealt[:], 0.0)
+        nc.gpsimd.memset(dealt_rows[:], 0.0)
         make_identity(nc, ident[:])
         warm = sb("warm", [P, 1], F32)
         nc.scalar.activation(warm[:], ident[:, 0:1], ACT.Sigmoid)
-        nc.gpsimd.tensor_copy(dealt[0:4, :].rearrange("v (t g i) -> v t g i", t=4, i=4),
-                              rows[0:4, :].rearrange("v (g t i) -> v t g i", t=4, i=4))
-        rows_ps = bank(7, "rows_ps")
-        for t in range(4):
-            nc.tensor.transpose(rows_ps[:, P * t : P * (t + 1)], dealt[:, P * t : P * (t + 1)], ident[:])
-        fac = sb("fac", [P, 16], F32)
-        nc.scalar.copy(fac[:].rearrange("p (v t) -> p v t", t=4), rows_ps[:].rearrange("p (t v) -> p v t", t=4)[:, 0:4, :])
-        GK, GQ, GI, GT = 0, 4, 8, 12
+        nc.gpsimd.tensor_copy(
+            dealt_rows[0:4, :].rearrange("v (t g i) -> v t g i", t=SLOTS, i=RUN),
+            factor_rows[0:4, :].rearrange("v (g t i) -> v t g i", t=SLOTS, i=RUN),
+        )
+        turned = bank(7, "turned")
+        for t in range(SLOTS):
+            nc.tensor.transpose(turned[:, P * t : P * (t + 1)], dealt_rows[:, P * t : P * (t + 1)], ident[:])
+        factors = sb("factors", [P, 16], F32)
+        nc.scalar.copy(
+            factors[:].rearrange("p (v t) -> p v t", t=SLOTS),
+            turned[:].rearrange("p (t v) -> p v t", t=SLOTS)[:, 0:4, :],
+        )
 
-        ko_w = sb("ko_w", [P, W], U32)
-        ko_s_list = sb("ko_s_list", [P, W], U8)
-        ko_s = sb("ko_s", [P, W], U8)
-        qo_w = sb("qo_w", [P, W], U32)
-        qo_s = sb("qo_s", [P, W], U8)
-        nc.vector.tensor_copy(ko_w[:].rearrange("p (t g i) -> p g t i", t=4, i=4), xw[:].indirect(offs_t[:]))
-        nc.vector.tensor_copy(qo_w[:], xw[:].indirect(qs_t[:]))
-        nc.vector.tensor_copy(ko_s_list[:], xs[:].indirect(offs_t[:]))
-        nc.vector.tensor_copy(qo_s[:], xs[:].indirect(qs_t[:]))
+        key_words = sb("key_words", [P, W], U32)
+        key_scales_listed = sb("key_scales_listed", [P, W], U8)
+        key_scales = sb("key_scales", [P, W], U8)
+        query_words = sb("query_words", [P, W], U32)
         nc.vector.tensor_copy(
-            ko_s[:].bitcast(I32).rearrange("p (t g) -> p t g", t=4),
-            ko_s_list[:].bitcast(I32).rearrange("p (g t) -> p t g", t=4),
+            key_words[:].rearrange("p (t g i) -> p g t i", t=SLOTS, i=RUN), table_words[:].indirect(offs_t[:])
+        )
+        nc.vector.tensor_copy(query_words[:], table_words[:].indirect(qs_t[:]))
+        nc.vector.tensor_copy(key_scales_listed[:], table_scales[:].indirect(offs_t[:]))
+        nc.vector.tensor_copy(
+            key_scales[:].bitcast(I32).rearrange("p (t g) -> p t g", t=SLOTS),
+            key_scales_listed[:].bitcast(I32).rearrange("p (g t) -> p t g", t=SLOTS),
         )
 
         def operand(name):
-            return (sb(name + "_b", [P, 4 * W], BF16), sb(name + "_w", [P, W], U32), sb(name + "_s", [P, W], U8))
+            return {
+                "values": sb(name + "_values", [P, SLOTS * W], BF16),
+                "words": sb(name + "_words", [P, W], U32),
+                "scales": sb(name + "_scales", [P, W], U8),
+                "row": 0,
+            }
 
-        def quant(op, c0, c1):
-            nc.vector.quantize_mx(out=op[1][:, c0:c1].bitcast(FP8X4), scales=op[2][:, c0:c1], in_=op[0][:, 4 * c0 : 4 * c1])
+        def values(op, c0, c1):
+            return op["values"][:, SLOTS * c0 : SLOTS * c1]
 
-        def mm(o, lhs, l0, rhs, r0, r1):
-            nc.tensor.matmul_mx(out=o, lhsT=lhs[1][:, l0 : l0 + P].bitcast(FP8X4), lhsT_scale=lhs[2][:, l0 : l0 + P],
-                                rhs=rhs[1][:, r0:r1].bitcast(FP8X4), rhs_scale=rhs[2][:, r0:r1], start=True, stop=True)
+        def quantise(op, c0, c1):
+            nc.vector.quantize_mx(
+                out=op["words"][:, c0:c1].bitcast(FP8X4), scales=op["scales"][:, c0:c1], in_=values(op, c0, c1)
+            )
 
-        def cast_dealt(op, name):
-            nc.scalar.copy(op[0][:].rearrange("p (t g i j) -> p t g j i", t=4, i=4, j=4),
-                           raw[name][:].rearrange("p j (g t i) -> p t g j i", t=4, i=4))
+        def product(acc, lhs, tile, rhs, c0, c1):
+            cols = slice(P * tile, P * (tile + 1))
+            nc.tensor.matmul_mx(
+                out=acc,
+                lhsT=lhs["words"][:, cols].bitcast(FP8X4),
+                lhsT_scale=lhs["scales"][lhs["row"] : P, cols],
+                rhs=rhs["words"][:, c0:c1].bitcast(FP8X4),
+                rhs_scale=rhs["scales"][rhs["row"] : P, c0:c1],
+                start=True,
+                stop=True,
+            )
 
-        def cast_plain(op, name):
-            nc.scalar.copy(op[0][:].rearrange("p (c i j) -> p c j i", i=4, j=4),
-                           raw[name][:].rearrange("p j (c i) -> p c j i", i=4))
+        def quarter_product(b, name, lhs, rhs, c):
+            acc = bank(b, name)
+            for t in range(4):
+                product(acc[:, QUARTER * t : QUARTER * (t + 1)], lhs, t, rhs, QUARTER * c, QUARTER * (c + 1))
+            return acc
 
-        def direct(op, c, src, f0):
+        def half_product(b, name, lhs, rhs, h):
+            pair = [bank(b + u, "%s%d" % (name, u)) for u in range(2)]
+            for t in range(4):
+                product(pair[t // 2][:, HALF * (t % 2) : HALF * (t % 2 + 1)], lhs, t, rhs, HALF * h, HALF * (h + 1))
+            return pair
+
+        def cast_dealt(op, name, h):
+            groups = HALF // (SLOTS * RUN)
+            nc.scalar.copy(
+                op["values"][:].rearrange("p (t g i j) -> p t g j i", t=SLOTS, i=RUN, j=SLOTS)[
+                    :, :, groups * h : groups * (h + 1), :, :
+                ],
+                raw[name, h][:].rearrange("p j (g t i) -> p t g j i", t=SLOTS, i=RUN),
+            )
+
+        def cast_plain(op, name, h):
+            nc.scalar.copy(
+                values(op, HALF * h, HALF * (h + 1)).rearrange("p (c i j) -> p c j i", i=RUN, j=SLOTS),
+                raw[name, h][:].rearrange("p j (c i) -> p c j i", i=RUN),
+            )
+
+        def scale_from_bank(op, c, acc, first):
             nc.vector.tensor_tensor(
-                op[0][:, 4 * CH * c : 4 * CH * (c + 1)].rearrange("p (s t) -> p s t", t=4),
-                src,
-                fac[:, f0 : f0 + 4].unsqueeze(1).to_broadcast([P, CH, 4]),
+                values(op, QUARTER * c, QUARTER * (c + 1)).rearrange("p (c i t) -> p c t i", i=2, t=SLOTS),
+                acc[:].rearrange("p (t c i) -> p c t i", t=SLOTS, i=2),
+                factors[:, first : first + SLOTS].unsqueeze(1).unsqueeze(3).to_broadcast([P, QUARTER // 2, SLOTS, 2]),
                 ALU.mult,
             )
 
-        def weave(op, c0, c1, planes):
-            nc.vector.tensor_copy(op[0][:, 4 * c0 : 4 * c1].rearrange("p (c i t) -> p c t i", i=4, t=4),
-                                  planes.rearrange("p t (c i) -> p c t i", i=4))
+        def scaled_planes(pair, name, first):
+            planes = sb(name, [P, SLOTS, HALF], BF16)
+            for t in range(SLOTS):
+                nc.scalar.activation(
+                    planes[:, t, :],
+                    pair[t // 2][:, HALF * (t % 2) : HALF * (t % 2 + 1)],
+                    ACT.Copy,
+                    scale=factors[:, first + t : first + t + 1],
+                )
+            return planes
 
-        keys = (None, ko_w, ko_s)
-        quer = (None, qo_w, qo_s)
+        def weave(op, c0, c1, planes):
+            nc.vector.tensor_copy(
+                values(op, c0, c1).rearrange("p (c i t) -> p c t i", i=RUN, t=SLOTS),
+                planes[:].rearrange("p t (c i) -> p c t i", i=RUN),
+            )
+
+        keys = {"words": key_words, "scales": key_scales, "row": 4}
         w1q, w2q, wvq = operand("w1q"), operand("w2q"), operand("wvq")
         z, z2, zv, zp = operand("z"), operand("z2"), operand("zv"), operand("zp")
 
-        cast_dealt(w1q, "w1")
-        quant(w1q, 0, W)
-        cast_dealt(w2q, "w2")
-        kf = [bank(c, "kf%d" % c) for c in range(4)]
-        for c in range(4):
-            for t in range(4):
-                mm(kf[c][:, CH * t : CH * (t + 1)], w1q, P * t, keys, CH * c, CH * (c + 1))
-        direct(z, 0, kf[0][:].rearrange("p (t s) -> p s t", t=4), GK)
-        direct(z, 1, kf[1][:].rearrange("p (t s) -> p s t", t=4), GK)
-        quant(w2q, 0, W)
-        cast_plain(wvq, "wv")
-        direct(z, 2, kf[2][:].rearrange("p (t s) -> p s t", t=4), GK)
-        direct(z, 3, kf[3][:].rearrange("p (t s) -> p s t", t=4), GK)
-        z2_planes = []
-        for h in range(2):
-            pl = sb("z2_planes%d" % h, [P, 4, 256], BF16)
-            z2_planes.append(pl)
-            for u in range(2):
-                b = bank(4 + 2 * h + u, "qf%d%d" % (h, u))
-                for e in range(2):
-                    mm(b[:, 256 * e : 256 * (e + 1)], w2q, P * (2 * u + e), quer, 256 * h, 256 * (h + 1))
-                for e in range(2):
-                    t = 2 * u + e
-                    nc.scalar.activation(pl[:, t, :], b[:, 256 * e : 256 * (e + 1)], ACT.Copy, scale=fac[:, GQ + t : GQ + t + 1])
-        quant(wvq, 0, W)
-        quant(z, 0, W)
-        val = [bank(c, "val%d" % c) for c in range(4)]
-        for c in range(4):
-            for t in range(4):
-                mm(val[c][:, CH * t : CH * (t + 1)], keys, P * t, wvq, CH * c, CH * (c + 1))
-        weave(z2, 0, 256, z2_planes[0][:])
-        direct(zv, 0, val[0][:].rearrange("p (t s) -> p s t", t=4), GI)
-        quant(z2, 0, 256)
-        direct(zv, 1, val[1][:].rearrange("p (t s) -> p s t", t=4), GI)
-        weave(z2, 256, 512, z2_planes[1][:])
-        direct(zv, 2, val[2][:].rearrange("p (t s) -> p s t", t=4), GI)
-        quant(z2, 256, 512)
-        direct(zv, 3, val[3][:].rearrange("p (t s) -> p s t", t=4), GI)
+        cast_dealt(w1q, "w1", 0)
+        cast_dealt(w1q, "w1", 1)
+        quantise(w1q, 0, W)
+        query_scales = sb("query_scales", [P, W], U8, tag="w1q_values")
+        nc.vector.tensor_copy(query_scales[:], table_scales[:].indirect(qs_t[:]))
+        queries = {"words": query_words, "scales": query_scales, "row": 4}
+        cast_dealt(w2q, "w2", 0)
+        cast_dealt(w2q, "w2", 1)
+        kf = [quarter_product(c, "kf%d" % c, w1q, keys, c) for c in range(4)]
+        scale_from_bank(z, 0, kf[0], GK)
+        scale_from_bank(z, 1, kf[1], GK)
+        quantise(w2q, 0, W)
+        cast_plain(wvq, "wv", 0)
+        cast_plain(wvq, "wv", 1)
+        scale_from_bank(z, 2, kf[2], GK)
+        scale_from_bank(z, 3, kf[3], GK)
 
-        def scores(c):
-            b = bank(4 + c, "s%d" % c)
-            for t in range(4):
-                mm(b[:, CH * t : CH * (t + 1)], z, P * t, z2, CH * c, CH * (c + 1))
-            sg = sb("sg%d" % c, [P, W], F32)
-            if ZP_MODES[c] == "V":
-                nc.scalar.activation(sg[:].rearrange("p (s t) -> p s t", t=4), b[:].rearrange("p (t s) -> p s t", t=4), ACT.Sigmoid, scale=0.0625)
-                return sg
-            nc.scalar.activation(sg[:], b[:], ACT.Sigmoid, scale=0.0625)
-            pl = sb("zp_planes%d" % c, [P, 4, CH], BF16)
-            for t in range(4):
-                nc.scalar.activation(pl[:, t, :], sg[:, CH * t : CH * (t + 1)], ACT.Copy, scale=fac[:, GT + t : GT + t + 1])
-            return pl
+        z2_lo = scaled_planes(half_product(4, "qf_lo", w2q, queries, 0), "z2_lo", GQ)
+        quantise(wvq, 0, W)
+        quantise(z, 0, W)
+        z2_hi = scaled_planes(half_product(6, "qf_hi", w2q, queries, 1), "z2_hi", GQ)
+        val_lo = [quarter_product(c, "val%d" % c, keys, wvq, c) for c in range(2)]
+        val_hi = half_product(2, "val_hi", keys, wvq, 1)
+        weave(z2, 0, HALF, z2_lo)
+        scale_from_bank(zv, 0, val_lo[0], GI)
+        quantise(z2, 0, HALF)
+        scale_from_bank(zv, 1, val_lo[1], GI)
+        zv_hi = scaled_planes(val_hi, "zv_hi", GI)
 
-        def make_zp(c, src):
-            if ZP_MODES[c] == "V":
-                direct(zp, c, src[:].rearrange("p (s t) -> p s t", t=4), GT)
-            else:
-                weave(zp, CH * c, CH * (c + 1), src[:])
+        def sigmoid_planes(c):
+            s = quarter_product(4 + c, "s%d" % c, z, z2, c)
+            sig = sb("sig%d" % c, [P, W], F32)
+            nc.scalar.activation(sig[:], s[:], ACT.Sigmoid, scale=SIXTEENTH)
+            planes = sb("zp_planes%d" % c, [P, SLOTS, QUARTER], BF16)
+            for t in range(SLOTS):
+                nc.scalar.activation(
+                    planes[:, t, :],
+                    sig[:, QUARTER * t : QUARTER * (t + 1)],
+                    ACT.Copy,
+                    scale=factors[:, GT + t : GT + t + 1],
+                )
+            return planes
 
-        def finish(c):
-            b = bank(c, "o%d" % c)
-            for a in range(4):
-                mm(b[:, CH * a : CH * (a + 1)], zv, P * a, zp, CH * c, CH * (c + 1))
-            o = sb("o%d" % c, [P, 4, CH], F32)
-            nc.vector.scalar_tensor_tensor(o[:], b[:].rearrange("p (a v) -> p a v", a=4), 0.0625,
-                                           res_t[:, :, CH * c : CH * (c + 1)], ALU.mult, ALU.add)
-            nc.sync.dma_start(out.rearrange("(a p) v -> p a v", p=P)[:, :, CH * c : CH * (c + 1)], o[:])
+        def sigmoid_interleaved(c):
+            s = quarter_product(4 + c, "s%d" % c, z, z2, c)
+            sig = sb("sig%d" % c, [P, W], F32)
+            nc.scalar.activation(
+                sig[:].rearrange("p (v t) -> p v t", t=SLOTS),
+                s[:].rearrange("p (t v) -> p v t", t=SLOTS),
+                ACT.Sigmoid,
+                scale=SIXTEENTH,
+            )
+            return sig
 
-        made = [scores(c) for c in range(4)]
-        make_zp(0, made[0])
-        quant(zv, 0, W)
-        quant(zp, 0, CH)
-        for c in range(1, 4):
-            make_zp(c, made[c])
-            finish(c - 1)
-            quant(zp, CH * c, CH * (c + 1))
-        finish(3)
+        def scale_interleaved(c, sig):
+            nc.vector.tensor_tensor(
+                values(zp, QUARTER * c, QUARTER * (c + 1)).rearrange("p (v t) -> p v t", t=SLOTS),
+                sig[:].rearrange("p (v t) -> p v t", t=SLOTS),
+                factors[:, GT : GT + SLOTS].unsqueeze(1).to_broadcast([P, QUARTER, SLOTS]),
+                ALU.mult,
+            )
+
+        zp0_planes = sigmoid_planes(0)
+        sig1 = sigmoid_interleaved(1)
+        weave(z2, HALF, W, z2_hi)
+        quantise(zv, 0, HALF)
+        quantise(z2, HALF, W)
+        weave(zv, HALF, W, zv_hi)
+        quantise(zv, HALF, W)
+        zp2_planes = sigmoid_planes(2)
+        sig3 = sigmoid_interleaved(3)
+        weave(zp, 0, QUARTER, zp0_planes)
+        scale_interleaved(1, sig1)
+        quantise(zp, 0, HALF)
+        scale_interleaved(3, sig3)
+        quantise(zp, 3 * QUARTER, W)
+        weave(zp, HALF, 3 * QUARTER, zp2_planes)
+        quantise(zp, HALF, 3 * QUARTER)
+
+        out_tiles = out.rearrange("(a p) v -> p a v", p=P)
+
+        def add_res_and_store(name, acc, tiles, cols):
+            result = sb(name, list(acc.shape), F32)
+            nc.vector.scalar_tensor_tensor(result[:], acc, SIXTEENTH, res_t[:, tiles, cols], ALU.mult, ALU.add)
+            nc.sync.dma_start(out_tiles[:, tiles, cols], result[:])
+
+        acc_lo = half_product(0, "acc_lo", zv, zp, 0)
+        lo = slice(0, HALF)
+        scaled = sb("scaled", [P, 2, HALF], F32)
+        summed = sb("summed", [P, 2, HALF], F32)
+        nc.scalar.activation(scaled[:], acc_lo[0][:].rearrange("p (a v) -> p a v", a=2), ACT.Copy, scale=SIXTEENTH)
+        for a in range(2):
+            nc.gpsimd.tensor_tensor(summed[:, a, :], scaled[:, a, :], res_t[:, a, lo], ALU.add)
+            nc.scalar.dma_start(out_tiles[:, a, lo], summed[:, a, :])
+        add_res_and_store("out_lo", acc_lo[1][:].rearrange("p (a v) -> p a v", a=2), slice(2, 4), lo)
+
+        acc3 = quarter_product(3, "acc3", zv, zp, 3)[:].rearrange("p (a v) -> p a v", a=4)
+        add_res_and_store("out3", acc3, slice(0, 4), slice(3 * QUARTER, W))
+        acc2 = quarter_product(2, "acc2", zv, zp, 2)[:].rearrange("p (a v) -> p a v", a=4)
+        for u in range(2):
+            tiles = slice(2 * u, 2 * u + 2)
+            add_res_and_store("out2_%d" % u, acc2[:, tiles, :], tiles, slice(HALF, 3 * QUARTER))

from contextlib import ExitStack

import concourse.mybir as mybir
from concourse.masks import make_identity

F32 = mybir.dt.float32
BF16 = mybir.dt.bfloat16
I32 = mybir.dt.int32
U32 = mybir.dt.uint32
U16 = mybir.dt.uint16
U8 = mybir.dt.uint8
FP8X4 = mybir.dt.float8_e4m3fn_x4
ACT = mybir.ActivationFunctionType
ALU = mybir.AluOpType

P = 128
TOKENS = 2048
W = 512
SLOTS = 4
RUN = 4
HALF = W // 2
QUARTER = W // 4
SIXTEENTH = 0.0625
FLOPS = 5 * 2 * W * W * W

GK, GQ, GI, GT = 0, 4, 8, 12


def tile_picked_listattn_sigmoid_p_kernel(
    tc, x_words, x_scales, w1, w2, gk, gq, wv, gi, res, gt, offs, qs, out
):
    nc = tc.nc
    with ExitStack() as ctx:
        keep = ctx.enter_context(tc.tile_pool(name="keep", bufs=1))
        psum = ctx.enter_context(tc.psum_pool(name="psum", bufs=1))

        def sb(name, shape, dtype, tag=None):
            return keep.tile(shape, dtype, name=name, tag=tag or name, align_bytes=64)

        def bank(b, name):
            return psum.tile([P, W], F32, name=name, tag="bank%d" % b)

        offs_t = sb("offs_t", [P, W // 16], U16)
        qs_t = sb("qs_t", [P, W // 16], U16)
        table_words = sb("table_words", [P, TOKENS], U32)
        table_scales = sb("table_scales", [P, TOKENS], U8)
        nc.vector.memset(table_scales[:].bitcast(I32), 0)
        nc.sync.dma_start(offs_t[:], offs)
        nc.sync.dma_start(qs_t[:], qs)
        nc.sync.dma_start(table_words[:].bitcast(I32), x_words[0].rearrange("p n t -> p (n t)").bitcast(I32))
        for q in range(4):
            nc.sync.dma_start(
                table_scales[32 * q + 4 : 32 * q + 8, :].bitcast(I32), x_scales[0][4 * q : 4 * q + 4, :].bitcast(I32)
            )
        factor_rows = sb("factor_rows", [P, W], F32)
        for v, vector in enumerate((gk, gq, gi, gt)):
            nc.scalar.dma_start(factor_rows[v : v + 1, :], vector.rearrange("k o -> o k"))
        raw = {}
        for name, w in (("w1", w1), ("w2", w2), ("wv", wv)):
            for h in range(2):
                raw[name, h] = sb("raw_%s%d" % (name, h), [P, SLOTS, HALF], F32)
                nc.sync.dma_start(
                    raw[name, h][:], w.rearrange("(p j) c -> p j c", j=SLOTS)[:, :, HALF * h : HALF * (h + 1)]
                )
        res_t = sb("res_t", [P, 4, W], F32)
        nc.sync.dma_start(res_t[:], res.rearrange("(a p) v -> p a v", p=P))

        dealt_rows = sb("dealt_rows", [P, W], F32)
        ident = sb("ident", [P, P], F32)
        nc.gpsimd.memset(dealt_rows[:], 0.0)
        make_identity(nc, ident[:])
        warm = sb("warm", [P, 1], F32)
        nc.scalar.activation(warm[:], ident[:, 0:1], ACT.Sigmoid)
        nc.gpsimd.tensor_copy(
            dealt_rows[0:4, :].rearrange("v (t g i) -> v t g i", t=SLOTS, i=RUN),
            factor_rows[0:4, :].rearrange("v (g t i) -> v t g i", t=SLOTS, i=RUN),
        )
        turned = bank(7, "turned")
        for t in range(SLOTS):
            nc.tensor.transpose(turned[:, P * t : P * (t + 1)], dealt_rows[:, P * t : P * (t + 1)], ident[:])
        factors = sb("factors", [P, 16], F32)
        nc.scalar.copy(
            factors[:].rearrange("p (v t) -> p v t", t=SLOTS),
            turned[:].rearrange("p (t v) -> p v t", t=SLOTS)[:, 0:4, :],
        )

        key_words = sb("key_words", [P, W], U32)
        key_scales_listed = sb("key_scales_listed", [P, W], U8)
        key_scales = sb("key_scales", [P, W], U8)
        query_words = sb("query_words", [P, W], U32)
        nc.vector.tensor_copy(
            key_words[:].rearrange("p (t g i) -> p g t i", t=SLOTS, i=RUN), table_words[:].indirect(offs_t[:])
        )
        nc.vector.tensor_copy(query_words[:], table_words[:].indirect(qs_t[:]))
        nc.vector.tensor_copy(key_scales_listed[:], table_scales[:].indirect(offs_t[:]))
        nc.vector.tensor_copy(
            key_scales[:].bitcast(I32).rearrange("p (t g) -> p t g", t=SLOTS),
            key_scales_listed[:].bitcast(I32).rearrange("p (g t) -> p t g", t=SLOTS),
        )

        def operand(name):
            return {
                "values": sb(name + "_values", [P, SLOTS * W], BF16),
                "words": sb(name + "_words", [P, W], U32),
                "scales": sb(name + "_scales", [P, W], U8),
                "row": 0,
            }

        def values(op, c0, c1):
            return op["values"][:, SLOTS * c0 : SLOTS * c1]

        def quantise(op, c0, c1):
            nc.vector.quantize_mx(
                out=op["words"][:, c0:c1].bitcast(FP8X4), scales=op["scales"][:, c0:c1], in_=values(op, c0, c1)
            )

        def product(acc, lhs, tile, rhs, c0, c1):
            cols = slice(P * tile, P * (tile + 1))
            nc.tensor.matmul_mx(
                out=acc,
                lhsT=lhs["words"][:, cols].bitcast(FP8X4),
                lhsT_scale=lhs["scales"][lhs["row"] : P, cols],
                rhs=rhs["words"][:, c0:c1].bitcast(FP8X4),
                rhs_scale=rhs["scales"][rhs["row"] : P, c0:c1],
                start=True,
                stop=True,
            )

        def quarter_product(b, name, lhs, rhs, c):
            acc = bank(b, name)
            for t in range(4):
                product(acc[:, QUARTER * t : QUARTER * (t + 1)], lhs, t, rhs, QUARTER * c, QUARTER * (c + 1))
            return acc

        def half_product(b, name, lhs, rhs, h):
            pair = [bank(b + u, "%s%d" % (name, u)) for u in range(2)]
            for t in range(4):
                product(pair[t // 2][:, HALF * (t % 2) : HALF * (t % 2 + 1)], lhs, t, rhs, HALF * h, HALF * (h + 1))
            return pair

        def cast_dealt(op, name, h):
            groups = HALF // (SLOTS * RUN)
            nc.scalar.copy(
                op["values"][:].rearrange("p (t g i j) -> p t g j i", t=SLOTS, i=RUN, j=SLOTS)[
                    :, :, groups * h : groups * (h + 1), :, :
                ],
                raw[name, h][:].rearrange("p j (g t i) -> p t g j i", t=SLOTS, i=RUN),
            )

        def cast_plain(op, name, h):
            nc.scalar.copy(
                values(op, HALF * h, HALF * (h + 1)).rearrange("p (c i j) -> p c j i", i=RUN, j=SLOTS),
                raw[name, h][:].rearrange("p j (c i) -> p c j i", i=RUN),
            )

        def scale_from_bank(op, c, acc, first):
            nc.vector.tensor_tensor(
                values(op, QUARTER * c, QUARTER * (c + 1)).rearrange("p (c i t) -> p c t i", i=2, t=SLOTS),
                acc[:].rearrange("p (t c i) -> p c t i", t=SLOTS, i=2),
                factors[:, first : first + SLOTS].unsqueeze(1).unsqueeze(3).to_broadcast([P, QUARTER // 2, SLOTS, 2]),
                ALU.mult,
            )

        def scaled_planes(pair, name, first):
            planes = sb(name, [P, SLOTS, HALF], BF16)
            for t in range(SLOTS):
                nc.scalar.activation(
                    planes[:, t, :],
                    pair[t // 2][:, HALF * (t % 2) : HALF * (t % 2 + 1)],
                    ACT.Copy,
                    scale=factors[:, first + t : first + t + 1],
                )
            return planes

        def weave(op, c0, c1, planes):
            nc.vector.tensor_copy(
                values(op, c0, c1).rearrange("p (c i t) -> p c t i", i=RUN, t=SLOTS),
                planes[:].rearrange("p t (c i) -> p c t i", i=RUN),
            )

        keys = {"words": key_words, "scales": key_scales, "row": 4}
        w1q, w2q, wvq = operand("w1q"), operand("w2q"), operand("wvq")
        z, z2, zv, zp = operand("z"), operand("z2"), operand("zv"), operand("zp")

        cast_dealt(w1q, "w1", 0)
        cast_dealt(w1q, "w1", 1)
        quantise(w1q, 0, W)
        query_scales = sb("query_scales", [P, W], U8, tag="w1q_values")
        nc.vector.tensor_copy(query_scales[:], table_scales[:].indirect(qs_t[:]))
        queries = {"words": query_words, "scales": query_scales, "row": 4}
        cast_dealt(w2q, "w2", 0)
        cast_dealt(w2q, "w2", 1)
        kf = [quarter_product(c, "kf%d" % c, w1q, keys, c) for c in range(4)]
        scale_from_bank(z, 0, kf[0], GK)
        scale_from_bank(z, 1, kf[1], GK)
        quantise(w2q, 0, W)
        cast_plain(wvq, "wv", 0)
        cast_plain(wvq, "wv", 1)
        scale_from_bank(z, 2, kf[2], GK)
        scale_from_bank(z, 3, kf[3], GK)

        z2_lo = scaled_planes(half_product(4, "qf_lo", w2q, queries, 0), "z2_lo", GQ)
        quantise(wvq, 0, W)
        quantise(z, 0, W)
        z2_hi = scaled_planes(half_product(6, "qf_hi", w2q, queries, 1), "z2_hi", GQ)
        val_lo = [quarter_product(c, "val%d" % c, keys, wvq, c) for c in range(2)]
        val_hi = half_product(2, "val_hi", keys, wvq, 1)
        weave(z2, 0, HALF, z2_lo)
        scale_from_bank(zv, 0, val_lo[0], GI)
        quantise(z2, 0, HALF)
        scale_from_bank(zv, 1, val_lo[1], GI)
        zv_hi = scaled_planes(val_hi, "zv_hi", GI)

        def sigmoid_planes(c):
            s = quarter_product(4 + c, "s%d" % c, z, z2, c)
            sig = sb("sig%d" % c, [P, W], F32)
            nc.scalar.activation(sig[:], s[:], ACT.Sigmoid, scale=SIXTEENTH)
            planes = sb("zp_planes%d" % c, [P, SLOTS, QUARTER], BF16)
            for t in range(SLOTS):
                nc.scalar.activation(
                    planes[:, t, :],
                    sig[:, QUARTER * t : QUARTER * (t + 1)],
                    ACT.Copy,
                    scale=factors[:, GT + t : GT + t + 1],
                )
            return planes

        def sigmoid_interleaved(c):
            s = quarter_product(4 + c, "s%d" % c, z, z2, c)
            sig = sb("sig%d" % c, [P, W], F32)
            nc.scalar.activation(
                sig[:].rearrange("p (v t) -> p v t", t=SLOTS),
                s[:].rearrange("p (t v) -> p v t", t=SLOTS),
                ACT.Sigmoid,
                scale=SIXTEENTH,
            )
            return sig

        def scale_interleaved(c, sig):
            nc.vector.tensor_tensor(
                values(zp, QUARTER * c, QUARTER * (c + 1)).rearrange("p (v t) -> p v t", t=SLOTS),
                sig[:].rearrange("p (v t) -> p v t", t=SLOTS),
                factors[:, GT : GT + SLOTS].unsqueeze(1).to_broadcast([P, QUARTER, SLOTS]),
                ALU.mult,
            )

        zp0_planes = sigmoid_planes(0)
        sig1 = sigmoid_interleaved(1)
        weave(z2, HALF, W, z2_hi)
        quantise(zv, 0, HALF)
        quantise(z2, HALF, W)
        weave(zv, HALF, W, zv_hi)
        quantise(zv, HALF, W)
        zp2_planes = sigmoid_planes(2)
        sig3 = sigmoid_interleaved(3)
        weave(zp, 0, QUARTER, zp0_planes)
        scale_interleaved(1, sig1)
        quantise(zp, 0, HALF)
        scale_interleaved(3, sig3)
        quantise(zp, 3 * QUARTER, W)
        weave(zp, HALF, 3 * QUARTER, zp2_planes)
        quantise(zp, HALF, 3 * QUARTER)

        out_tiles = out.rearrange("(a p) v -> p a v", p=P)

        def add_res_and_store(name, acc, tiles, cols):
            result = sb(name, list(acc.shape), F32)
            nc.vector.scalar_tensor_tensor(result[:], acc, SIXTEENTH, res_t[:, tiles, cols], ALU.mult, ALU.add)
            nc.sync.dma_start(out_tiles[:, tiles, cols], result[:])

        acc_lo = half_product(0, "acc_lo", zv, zp, 0)
        lo = slice(0, HALF)
        scaled = sb("scaled", [P, 2, HALF], F32)
        summed = sb("summed", [P, 2, HALF], F32)
        nc.scalar.activation(scaled[:], acc_lo[0][:].rearrange("p (a v) -> p a v", a=2), ACT.Copy, scale=SIXTEENTH)
        for a in range(2):
            nc.gpsimd.tensor_tensor(summed[:, a, :], scaled[:, a, :], res_t[:, a, lo], ALU.add)
            nc.scalar.dma_start(out_tiles[:, a, lo], summed[:, a, :])
        add_res_and_store("out_lo", acc_lo[1][:].rearrange("p (a v) -> p a v", a=2), slice(2, 4), lo)

        acc3 = quarter_product(3, "acc3", zv, zp, 3)[:].rearrange("p (a v) -> p a v", a=4)
        add_res_and_store("out3", acc3, slice(0, 4), slice(3 * QUARTER, W))
        acc2 = quarter_product(2, "acc2", zv, zp, 2)[:].rearrange("p (a v) -> p a v", a=4)
        for u in range(2):
            tiles = slice(2 * u, 2 * u + 2)
            add_res_and_store("out2_%d" % u, acc2[:, tiles, :], tiles, slice(HALF, 3 * QUARTER))
